import numpy as np
import ml_dtypes


def mxq(x, axis, fmt="e4m3"):
    dtype, down = {"e4m3": (ml_dtypes.float8_e4m3fn, 7), "e5m2": (ml_dtypes.float8_e5m2, 14)}[fmt]
    v = np.moveaxis(np.asarray(x, np.float32).astype(ml_dtypes.bfloat16).astype(np.float64), axis, -1)
    blocks = v.reshape(v.shape[:-1] + (-1, 32))
    amax = np.abs(blocks).max(-1, keepdims=True)
    byte = np.maximum(np.where(amax > 0, np.frexp(amax)[1] - 1 + 127, 0) - down, 1)
    scale = np.exp2(byte - 127.0)
    codes = (blocks / scale).astype(np.float32).astype(dtype).astype(np.float64)
    return np.moveaxis((codes * scale).reshape(v.shape), -1, axis)


WIDE = False


def mx_kscale(k):
    if not WIDE:
        return np.ones(k)
    levels = np.array([10, -10, 5, -5, 0])
    if k % 512:
        return np.exp2(np.random.permutation(np.resize(levels, k // 32))).repeat(32)
    a = np.empty((k // 512, 16))
    for p in range(k // 512):
        a[p, :8] = np.random.permutation(np.resize(levels, 8))
        for g in range(8):
            far = levels[np.abs(levels - a[p, g]) >= 10]
            a[p, g + 8] = far[np.random.randint(len(far))]
    return np.exp2(a.ravel()).repeat(32)


def f64(x):
    return np.asarray(x).astype(np.float64)


def striped(idx):
    return np.tile(idx.reshape(-1, 16).T, (8, 1)).astype(np.uint16)


def unstriped(offs):
    return offs[:16].T.reshape(-1).astype(np.int64)


def striped8(idx):
    return np.concatenate([x.reshape(-1, 16).T for x in idx]).astype(np.uint16)


def runs(offs, k):
    lists = np.stack([offs[16 * r : 16 * r + 16].T.reshape(-1) for r in range(8)]).astype(np.int64)
    return lists[np.arange(k) % 512 // 64]


def pack_weight(w):
    k, n = w.shape
    w = f64(np.asarray(w, np.float32).astype(ml_dtypes.bfloat16)).reshape(k // 32, 32, n)
    amax = np.abs(w).max(1)
    byte = np.clip(np.where(amax > 0, np.frexp(amax)[1] - 1 + 127 - 7, 1), 1, 254)
    scaled = (w * np.exp2(127.0 - byte)[:, None, :]).reshape(k, n).astype(np.float32)
    words = np.ascontiguousarray(scaled.reshape(k // 512, 128, 4, n).transpose(0, 1, 3, 2)).astype(ml_dtypes.float8_e4m3fn).view(np.uint8)
    return words, np.ascontiguousarray(byte.astype(np.uint8).reshape(k // 512, 16, n))


def unpack_weight(words, scales):
    g, p, n, _ = words.shape
    vals = np.ascontiguousarray(words).view(ml_dtypes.float8_e4m3fn).astype(np.float64) * np.repeat(np.exp2(scales.astype(np.float64) - 127.0), 8, axis=1)[..., None]
    return vals.transpose(0, 1, 3, 2).reshape(g * 512, n)


def relu(v):
    return np.maximum(v, 0.0)


K, T, S, N, H, U = 512, 2048, 512, 512, 512, 1024


def setup_inputs():
    n = np.random.standard_normal
    s = mx_kscale(K)[:, None]
    u = mx_kscale(H)
    packed_xT = pack_weight(n((K, T)) * s)
    return {
        "x_words": packed_xT[0],
        "x_scales": packed_xT[1],
        "w1": (n((K, H)) / np.sqrt(K) / s).astype(np.float32),
        "gn": (np.random.uniform(0.5, 1.5, (H, 1)) * u[:, None]).astype(np.float32),
        "gm": (np.random.uniform(0.5, 1.5, (H, 1)) * u[:, None]).astype(np.float32),
        "w2": (n((H, N)) / np.sqrt(2 * H) / u[:, None]).astype(np.float32),
        "w3": (n((H, N)) / np.sqrt(2 * H) / u[:, None]).astype(np.float32),
        "offs": striped(np.random.permutation(T)[:S]),
        "n1": striped8(np.stack([np.random.permutation(S) for _ in range(8)])),
        "n2": striped8(np.stack([np.random.permutation(S) for _ in range(8)])),
        "n3": striped8(np.stack([np.random.permutation(S) for _ in range(8)])),
        "n4": striped8(np.stack([np.random.permutation(S) for _ in range(8)])),
        "n5": striped8(np.stack([np.random.permutation(S) for _ in range(8)])),
        "n6": striped8(np.stack([np.random.permutation(U)[:S] for _ in range(8)])),
        "n7": striped8(np.stack([np.random.permutation(S) for _ in range(8)])),
    }


def reference(x_words, x_scales, w1, gn, gm, w2, w3, offs, n1, n2, n3, n4, n5, n6, n7):
    xq = unpack_weight(x_words, x_scales)[:, unstriped(offs)]
    y = mxq(f64(w1), 0, "e4m3").T @ xq
    st = y + y[np.arange(H)[:, None], runs(n1, H)]
    z = f64(gn) * (st * (np.tanh(st[np.arange(H)[:, None], runs(n2, H)])))
    z2 = f64(gm) * (y + y[np.arange(H)[:, None], runs(n3, H)] - (np.maximum(y[np.arange(H)[:, None], runs(n4, H)], y[np.arange(H)[:, None], runs(n5, H)])))
    h = mxq(f64(w2), 0, "e4m3").T @ mxq(z, 0, "e4m3") + mxq(f64(w3), 0, "e4m3").T @ mxq(z2, 0, "e4m3")
    nw = h - (relu(h[np.arange(N)[:, None], runs(n7, N)]))
    out = np.zeros((N, U))
    out[np.arange(N)[:, None], runs(n6, N)] = nw
    return out

@@ -1,0 +1,229 @@
+from contextlib import ExitStack
+
+import concourse.mybir as mybir
+
+K, T, S, N, H, U = 512, 2048, 512, 512, 512, 1024
+FLOPS = 2 * S * (K * H + 2 * H * N)
+
+F32 = mybir.dt.float32
+BF16 = mybir.dt.bfloat16
+I32 = mybir.dt.int32
+U32 = mybir.dt.uint32
+U16 = mybir.dt.uint16
+U8 = mybir.dt.uint8
+FP8X4 = mybir.dt.float8_e4m3fn_x4
+ALU = mybir.AluOpType
+ACT = mybir.ActivationFunctionType
+
+P = 128
+PACK = 4
+HALF = S // 2
+COLS = HALF // 16
+
+
+def tile_picked_joinhopptrimpagez_none_p_kernel(tc, x_words, x_scales, w1, gn, gm, w2, w3, offs, n1, n2, n3, n4, n5, n6, n7, out):
+    nc = tc.nc
+    with ExitStack() as ctx:
+        keep = ctx.enter_context(tc.tile_pool(name="keep", bufs=1))
+        ring = ctx.enter_context(tc.tile_pool(name="ring", bufs=2))
+        psum = ctx.enter_context(tc.psum_pool(name="psum", bufs=8))
+
+        def load_list(src, name):
+            t = keep.tile([P, S // 16], U16, name=name)
+            nc.sync.dma_start(t[:], src)
+            return t
+
+        def load_weight(src, name):
+            t = keep.tile([P, PACK, H], F32, name=name)
+            nc.sync.dma_start(t[:], src.rearrange("(p j) c -> p j c", j=PACK))
+            return t
+
+        def load_gain(src, name):
+            t = keep.tile([P, PACK], F32, name=name)
+            nc.sync.dma_start(t[:], src.rearrange("(p t) o -> p (t o)", t=PACK))
+            return t
+
+        def deal_weight(copy, grouped, raw, m0, m1):
+            copy(
+                grouped[:].rearrange("p (t m j) -> p m j t", t=PACK, j=PACK)[:, m0:m1],
+                raw[:].rearrange("p j (m t) -> p m j t", t=PACK)[:, m0:m1],
+            )
+
+        def mx_tiles(name):
+            grouped = keep.tile([P, PACK * S], BF16, name=name + "_bf", align_bytes=64)
+            codes = keep.tile([P, S], U32, name=name + "_codes", align_bytes=64)
+            scales = keep.tile([P, S], U8, name=name + "_scales", align_bytes=64)
+            return grouped, codes, scales
+
+        def quantise(tiles, c0, c1):
+            grouped, codes, scales = tiles
+            nc.vector.quantize_mx(out=codes[:, c0:c1].bitcast(FP8X4), scales=scales[:, c0:c1], in_=grouped[:, PACK * c0 : PACK * c1])
+
+        def product(acc, w, t, codes, scales, c0, c1, start, stop):
+            nc.tensor.matmul_mx(
+                out=acc,
+                lhsT=w[1][:, t * P : (t + 1) * P].bitcast(FP8X4),
+                lhsT_scale=w[2][:, t * P : (t + 1) * P],
+                rhs=codes[:, c0:c1].bitcast(FP8X4),
+                rhs_scale=scales[:, c0:c1],
+                start=start,
+                stop=stop,
+            )
+
+        def woven(ap, c0, c1):
+            return ap.rearrange("p (c i t) -> p c t i", i=4, t=PACK)[:, c0 // 4 : c1 // 4]
+
+        def planes(ap, c0, c1):
+            return ap.rearrange("p t (c i) -> p c t i", i=4)[:, c0 // 4 : c1 // 4]
+
+        xs = keep.tile([P, T], U8, name="xs", align_bytes=64)
+        nc.vector.memset(xs[:].bitcast(I32), 0)
+        l_offs = load_list(offs, "offs")
+        w1_raw = load_weight(w1, "w1_raw")
+        xw = keep.tile([P, T], I32, name="xw", align_bytes=64)
+        nc.sync.dma_start(xw[:], x_words[0].rearrange("p c r -> p (c r)").bitcast(I32))
+        for q in range(4):
+            nc.scalar.dma_start(xs[32 * q : 32 * q + 4, :].bitcast(I32), x_scales[0, 4 * q : 4 * q + 4, :].bitcast(I32))
+        l3 = load_list(n3, "n3")
+        l1 = load_list(n1, "n1")
+        l4 = load_list(n4, "n4")
+        l5 = load_list(n5, "n5")
+        l2 = load_list(n2, "n2")
+        gn_t = load_gain(gn, "gn")
+        gm_t = load_gain(gm, "gm")
+        w3_raw = load_weight(w3, "w3_raw")
+        w2_raw = load_weight(w2, "w2_raw")
+        l7 = load_list(n7, "n7")
+        l6 = load_list(n6, "n6")
+
+        y_win = [keep.tile([P, 2 * S], F32, name="y_win%d" % t) for t in range(PACK)]
+        y_last = keep.tile([P, S], F32, name="y_last")
+        y_plain = [y_win[t + 1][:, S:] for t in range(PACK - 1)] + [y_last[:]]
+        r_win = [keep.tile([P, 2 * S], F32, name="r_win%d" % t) for t in range(PACK)]
+        h_last = keep.tile([P, S], F32, name="h_last")
+        h_plain = [r_win[t + 1][:, S:] for t in range(PACK - 1)] + [h_last[:]]
+        s_win = [keep.tile([P, 2 * S], F32, name="s_win%d" % t) for t in range(PACK)]
+        page = [keep.tile([P, U], F32, name="page%d" % t) for t in range(PACK)]
+
+        nc.vector.memset(y_win[0][:, S:], 0.0)
+        warm = keep.tile([P, 1], F32, name="warm")
+        nc.scalar.activation(warm[:], y_win[0][:, S : S + 1], ACT.Sigmoid)
+        nc.vector.memset(r_win[0][:, S:], 0.0)
+        for t in range(PACK):
+            nc.vector.memset(page[t][:], 0.0)
+
+        xg_scales = keep.tile([P, S], U8, name="xg_scales", align_bytes=64)
+        nc.vector.tensor_copy(xg_scales[:], xs[:].indirect(l_offs[:]))
+
+        w1q = mx_tiles("w1")
+        deal_weight(nc.vector.tensor_copy, w1q[0], w1_raw, 0, 80)
+        deal_weight(nc.scalar.copy, w1q[0], w1_raw, 80, 128)
+        quantise(w1q, 0, S)
+
+        xg = keep.tile([P, S], U32, name="xg", align_bytes=64)
+        for c in range(2):
+            nc.vector.tensor_copy(xg[:, c * HALF : (c + 1) * HALF], xw[:].bitcast(U32).indirect(l_offs[:, c * COLS : (c + 1) * COLS]))
+
+        gn2 = keep.tile([P, PACK], F32, name="gn2")
+        gn_neg = keep.tile([P, PACK], F32, name="gn_neg")
+        gm_neg = keep.tile([P, PACK], F32, name="gm_neg")
+        nc.gpsimd.tensor_scalar(gn2[:], gn_t[:], 2.0, 0.0, ALU.mult, ALU.add)
+        nc.gpsimd.tensor_scalar(gn_neg[:], gn_t[:], -1.0, 0.0, ALU.mult, ALU.add)
+        nc.gpsimd.tensor_scalar(gm_neg[:], gm_t[:], -1.0, 0.0, ALU.mult, ALU.add)
+
+        for c in range(2):
+            cols = slice(c * HALF, (c + 1) * HALF)
+            acc = psum.tile([P, HALF], F32, name="acc")
+            product(acc[:], w1q, 0, xg, xg_scales, c * HALF, (c + 1) * HALF, True, True)
+            nc.scalar.copy(y_win[0][:, cols], acc[:])
+            nc.scalar.copy(y_plain[0][:, cols], acc[:])
+        for t in range(1, PACK):
+            acc = psum.tile([P, S], F32, name="acc")
+            product(acc[:], w1q, t, xg, xg_scales, 0, S, True, True)
+            nc.scalar.copy(y_win[t][:, :S], acc[:])
+            nc.scalar.copy(y_plain[t], acc[:])
+
+        w2q = mx_tiles("w2")
+        w3q = mx_tiles("w3")
+        zq = mx_tiles("z")
+        z2q = mx_tiles("z2")
+        gate = keep.tile([P, PACK, S], F32, name="gate")
+        st = keep.tile([P, PACK, S], F32, name="st")
+        z2 = keep.tile([P, PACK, S], F32, name="z2")
+
+        def near(t, c0=0, c1=S):
+            nc.vector.tensor_tensor(s_win[t][:, S + c0 : S + c1], y_win[t][:].indirect(l3[:, c0 // 16 : c1 // 16]), y_plain[t][:, c0:c1], ALU.add)
+
+        def rest(t):
+            nc.vector.tensor_tensor(s_win[t][:, :S], y_win[t][:].indirect(l1[:]), y_plain[t], ALU.add)
+            q4 = ring.tile([P, S], F32, name="q4")
+            q5 = ring.tile([P, S], F32, name="q5")
+            nc.vector.tensor_tensor(q4[:], y_win[t][:].indirect(l4[:]), s_win[t][:, S:], ALU.subtract)
+            nc.vector.tensor_tensor(q5[:], y_win[t][:].indirect(l5[:]), s_win[t][:, S:], ALU.subtract)
+            sig = ring.tile([P, S], F32, name="sig")
+            nc.scalar.activation(sig[:], s_win[t][:].indirect(l2[:]), ACT.Sigmoid, scale=2.0)
+            nc.scalar.activation(gate[:, t, :], sig[:], ACT.Identity, scale=gn2[:, t : t + 1], bias=gn_neg[:, t : t + 1])
+            nc.scalar.copy(st[:, t, :], s_win[t][:, :S])
+            return q4, q5
+
+        def larger(t, q4, q5):
+            big = ring.tile([P, S], F32, name="big")
+            nc.vector.tensor_tensor(big[:], q4[:], q5[:], ALU.max)
+            nc.scalar.activation(z2[:, t, :], big[:], ACT.Copy, scale=gm_neg[:, t : t + 1])
+
+        near(0, 0, HALF)
+        near(0, HALF, S)
+        for t in range(PACK):
+            q4, q5 = rest(t)
+            if t + 1 < PACK:
+                near(t + 1)
+            larger(t, q4, q5)
+            if t == 0:
+                deal_weight(nc.scalar.copy, w3q[0], w3_raw, 0, P)
+            if t == 1:
+                quantise(w3q, 0, S)
+                deal_weight(nc.scalar.copy, w2q[0], w2_raw, 0, P)
+            if t == 2:
+                quantise(w2q, 0, S)
+
+        for c in range(2):
+            c0, c1 = c * HALF, (c + 1) * HALF
+            nc.scalar.copy(woven(z2q[0][:], c0, c1), planes(z2[:], c0, c1))
+        for c in range(2):
+            c0, c1 = c * HALF, (c + 1) * HALF
+            nc.vector.tensor_tensor(woven(zq[0][:], c0, c1), planes(gate[:], c0, c1), planes(st[:], c0, c1), ALU.mult)
+        for c in range(2):
+            c0, c1 = c * HALF, (c + 1) * HALF
+            quantise(zq, c0, c1)
+            quantise(z2q, c0, c1)
+
+        acc_h = [[psum.tile([P, HALF], F32, name="acc") for c in range(2)] for t in range(PACK)]
+        for c in range(2):
+            for t in range(PACK):
+                product(acc_h[t][c][:], w2q, t, zq[1], zq[2], c * HALF, (c + 1) * HALF, True, False)
+                product(acc_h[t][c][:], w3q, t, z2q[1], z2q[2], c * HALF, (c + 1) * HALF, False, True)
+
+        out_rows = out.rearrange("(p t) u -> p t u", t=PACK)
+
+        def leave(t):
+            for c in range(2):
+                nc.scalar.activation(r_win[t][:, c * HALF : (c + 1) * HALF], acc_h[t][c][:], ACT.Relu)
+            for c in range(2):
+                nc.scalar.copy(h_plain[t][:, c * HALF : (c + 1) * HALF], acc_h[t][c][:])
+
+        def fetch(t):
+            minus = ring.tile([P, S], F32, name="minus")
+            nc.vector.tensor_scalar(minus[:], r_win[t][:].indirect(l7[:]), -1.0, 0.0, ALU.mult, ALU.add)
+            return minus
+
+        def put(t, minus):
+            nc.vector.tensor_tensor(page[t][:].indirect(l6[:]), h_plain[t], minus[:], ALU.add)
+            nc.sync.dma_start(out_rows[:, t, :], page[t][:])
+
+        for t in range(PACK):
+            leave(t)
+        minus = fetch(0)
+        for t in range(PACK):
+            ahead = fetch(t + 1) if t + 1 < PACK else None
+            put(t, minus)
+            minus = ahead

@@ -49,23 +49,23 @@ def tile_picked_joinhopptrimpagez_none_p_kernel(tc, x_words, x_scales, w1, gn, g
                 raw[:].rearrange("p j (m t) -> p m j t", t=PACK)[:, m0:m1],
             )
 
-        def mx_tiles(name):
+        def mx_tiles(name, scales_tag=None):
             grouped = keep.tile([P, PACK * S], BF16, name=name + "_bf", align_bytes=64)
             codes = keep.tile([P, S], U32, name=name + "_codes", align_bytes=64)
-            scales = keep.tile([P, S], U8, name=name + "_scales", align_bytes=64)
+            scales = keep.tile([P, S], U8, name=scales_tag or name + "_scales", align_bytes=64)
             return grouped, codes, scales
 
         def quantise(tiles, c0, c1):
             grouped, codes, scales = tiles
             nc.vector.quantize_mx(out=codes[:, c0:c1].bitcast(FP8X4), scales=scales[:, c0:c1], in_=grouped[:, PACK * c0 : PACK * c1])
 
-        def product(acc, w, t, codes, scales, c0, c1, start, stop):
+        def product(acc, w, t, codes, scales, start, stop):
             nc.tensor.matmul_mx(
                 out=acc,
                 lhsT=w[1][:, t * P : (t + 1) * P].bitcast(FP8X4),
                 lhsT_scale=w[2][:, t * P : (t + 1) * P],
-                rhs=codes[:, c0:c1].bitcast(FP8X4),
-                rhs_scale=scales[:, c0:c1],
+                rhs=codes.bitcast(FP8X4),
+                rhs_scale=scales,
                 start=start,
                 stop=stop,
             )
@@ -77,14 +77,14 @@ def tile_picked_joinhopptrimpagez_none_p_kernel(tc, x_words, x_scales, w1, gn, g
             return ap.rearrange("p t (c i) -> p c t i", i=4)[:, c0 // 4 : c1 // 4]
 
         xs = keep.tile([P, T], U8, name="xs", align_bytes=64)
-        nc.vector.memset(xs[:].bitcast(I32), 0)
-        l_offs = load_list(offs, "offs")
+        nc.gpsimd.memset(xs[:].bitcast(I32), 0)
         w1_raw = load_weight(w1, "w1_raw")
+        l_offs = load_list(offs, "offs")
+        l3 = load_list(n3, "n3")
+        for q in range(4):
+            nc.sync.dma_start(xs[32 * q : 32 * q + 4, :].bitcast(I32), x_scales[0, 4 * q : 4 * q + 4, :].bitcast(I32))
         xw = keep.tile([P, T], I32, name="xw", align_bytes=64)
         nc.sync.dma_start(xw[:], x_words[0].rearrange("p c r -> p (c r)").bitcast(I32))
-        for q in range(4):
-            nc.scalar.dma_start(xs[32 * q : 32 * q + 4, :].bitcast(I32), x_scales[0, 4 * q : 4 * q + 4, :].bitcast(I32))
-        l3 = load_list(n3, "n3")
         l1 = load_list(n1, "n1")
         l4 = load_list(n4, "n4")
         l5 = load_list(n5, "n5")
@@ -99,50 +99,53 @@ def tile_picked_joinhopptrimpagez_none_p_kernel(tc, x_words, x_scales, w1, gn, g
         y_win = [keep.tile([P, 2 * S], F32, name="y_win%d" % t) for t in range(PACK)]
         y_last = keep.tile([P, S], F32, name="y_last")
         y_plain = [y_win[t + 1][:, S:] for t in range(PACK - 1)] + [y_last[:]]
-        r_win = [keep.tile([P, 2 * S], F32, name="r_win%d" % t) for t in range(PACK)]
-        h_last = keep.tile([P, S], F32, name="h_last")
-        h_plain = [r_win[t + 1][:, S:] for t in range(PACK - 1)] + [h_last[:]]
+        r_win = y_win
+        h_plain = y_plain
         s_win = [keep.tile([P, 2 * S], F32, name="s_win%d" % t) for t in range(PACK)]
-        page = [keep.tile([P, U], F32, name="page%d" % t) for t in range(PACK)]
+        page = [keep.tile([P, U], F32, name="page%d" % t) for t in range(2)]
 
-        nc.vector.memset(y_win[0][:, S:], 0.0)
+        nc.gpsimd.memset(y_win[0][:, S:], 0.0)
         warm = keep.tile([P, 1], F32, name="warm")
         nc.scalar.activation(warm[:], y_win[0][:, S : S + 1], ACT.Sigmoid)
-        nc.vector.memset(r_win[0][:, S:], 0.0)
-        for t in range(PACK):
-            nc.vector.memset(page[t][:], 0.0)
-
+        w1q = mx_tiles("w1", "xs")
+        deal_weight(nc.vector.tensor_copy, w1q[0], w1_raw, 0, 40)
+        deal_weight(nc.scalar.copy, w1q[0], w1_raw, 40, 128)
         xg_scales = keep.tile([P, S], U8, name="xg_scales", align_bytes=64)
         nc.vector.tensor_copy(xg_scales[:], xs[:].indirect(l_offs[:]))
-
-        w1q = mx_tiles("w1")
-        deal_weight(nc.vector.tensor_copy, w1q[0], w1_raw, 0, 80)
-        deal_weight(nc.scalar.copy, w1q[0], w1_raw, 80, 128)
         quantise(w1q, 0, S)
 
-        xg = keep.tile([P, S], U32, name="xg", align_bytes=64)
+        xg = [keep.tile([P, HALF], U32, name=name, align_bytes=64) for name in ("w1_bf", "xg1")]
         for c in range(2):
-            nc.vector.tensor_copy(xg[:, c * HALF : (c + 1) * HALF], xw[:].bitcast(U32).indirect(l_offs[:, c * COLS : (c + 1) * COLS]))
+            nc.vector.tensor_copy(xg[c][:], xw[:].bitcast(U32).indirect(l_offs[:, c * COLS : (c + 1) * COLS]))
+
+        for t in range(2):
+            nc.gpsimd.memset(page[t][:], 0.0)
 
         gn2 = keep.tile([P, PACK], F32, name="gn2")
         gn_neg = keep.tile([P, PACK], F32, name="gn_neg")
         gm_neg = keep.tile([P, PACK], F32, name="gm_neg")
-        nc.gpsimd.tensor_scalar(gn2[:], gn_t[:], 2.0, 0.0, ALU.mult, ALU.add)
-        nc.gpsimd.tensor_scalar(gn_neg[:], gn_t[:], -1.0, 0.0, ALU.mult, ALU.add)
-        nc.gpsimd.tensor_scalar(gm_neg[:], gm_t[:], -1.0, 0.0, ALU.mult, ALU.add)
 
         for c in range(2):
             cols = slice(c * HALF, (c + 1) * HALF)
             acc = psum.tile([P, HALF], F32, name="acc")
-            product(acc[:], w1q, 0, xg, xg_scales, c * HALF, (c + 1) * HALF, True, True)
+            product(acc[:], w1q, 0, xg[c][:], xg_scales[:, cols], True, True)
             nc.scalar.copy(y_win[0][:, cols], acc[:])
             nc.scalar.copy(y_plain[0][:, cols], acc[:])
         for t in range(1, PACK):
             acc = psum.tile([P, S], F32, name="acc")
-            product(acc[:], w1q, t, xg, xg_scales, 0, S, True, True)
+            for c in range(2):
+                cols = slice(c * HALF, (c + 1) * HALF)
+                product(acc[:, cols], w1q, t, xg[c][:], xg_scales[:, cols], True, True)
             nc.scalar.copy(y_win[t][:, :S], acc[:])
             nc.scalar.copy(y_plain[t], acc[:])
 
+        for name in ("xw", "xg1"):
+            late = keep.tile([P, U], F32, name=name, align_bytes=64)
+            nc.gpsimd.memset(late[:], 0.0)
+            page.append(late)
+        nc.scalar.activation(gn2[:], gn_t[:], ACT.Copy, scale=2.0)
+        nc.scalar.activation(gn_neg[:], gn_t[:], ACT.Copy, scale=-1.0)
+        nc.scalar.activation(gm_neg[:], gm_t[:], ACT.Copy, scale=-1.0)
         w2q = mx_tiles("w2")
         w3q = mx_tiles("w3")
         zq = mx_tiles("z")
@@ -156,60 +159,80 @@ def tile_picked_joinhopptrimpagez_none_p_kernel(tc, x_words, x_scales, w1, gn, g
 
         def rest(t):
             nc.vector.tensor_tensor(s_win[t][:, :S], y_win[t][:].indirect(l1[:]), y_plain[t], ALU.add)
-            q4 = ring.tile([P, S], F32, name="q4")
-            q5 = ring.tile([P, S], F32, name="q5")
-            nc.vector.tensor_tensor(q4[:], y_win[t][:].indirect(l4[:]), s_win[t][:, S:], ALU.subtract)
-            nc.vector.tensor_tensor(q5[:], y_win[t][:].indirect(l5[:]), s_win[t][:, S:], ALU.subtract)
             sig = ring.tile([P, S], F32, name="sig")
             nc.scalar.activation(sig[:], s_win[t][:].indirect(l2[:]), ACT.Sigmoid, scale=2.0)
             nc.scalar.activation(gate[:, t, :], sig[:], ACT.Identity, scale=gn2[:, t : t + 1], bias=gn_neg[:, t : t + 1])
-            nc.scalar.copy(st[:, t, :], s_win[t][:, :S])
+            nc.sync.dma_start(st[:, t, :], s_win[t][:, :S])
+
+        def rivals(t, c0, c1, between=None):
+            q4 = ring.tile([P, c1 - c0], F32, name="q4")
+            q5 = ring.tile([P, c1 - c0], F32, name="q5")
+            nc.vector.tensor_tensor(q4[:], y_win[t][:].indirect(l4[:, c0 // 16 : c1 // 16]), s_win[t][:, S + c0 : S + c1], ALU.subtract)
+            if between:
+                between()
+            nc.vector.tensor_tensor(q5[:], y_win[t][:].indirect(l5[:, c0 // 16 : c1 // 16]), s_win[t][:, S + c0 : S + c1], ALU.subtract)
             return q4, q5
 
-        def larger(t, q4, q5):
-            big = ring.tile([P, S], F32, name="big")
+        def larger(t, c0, c1, q4, q5):
+            big = ring.tile([P, c1 - c0], F32, name="big")
             nc.vector.tensor_tensor(big[:], q4[:], q5[:], ALU.max)
-            nc.scalar.activation(z2[:, t, :], big[:], ACT.Copy, scale=gm_neg[:, t : t + 1])
+            nc.scalar.activation(z2[:, t, c0:c1], big[:], ACT.Copy, scale=gm_neg[:, t : t + 1])
 
         near(0, 0, HALF)
         near(0, HALF, S)
-        for t in range(PACK):
-            q4, q5 = rest(t)
-            if t + 1 < PACK:
-                near(t + 1)
-            larger(t, q4, q5)
+        for t in range(PACK - 1):
+            rest(t)
+            pair = rivals(t, 0, S)
+            near(t + 1)
+            larger(t, 0, S, *pair)
             if t == 0:
                 deal_weight(nc.scalar.copy, w3q[0], w3_raw, 0, P)
             if t == 1:
-                quantise(w3q, 0, S)
+                quantise(w3q, 0, P)
                 deal_weight(nc.scalar.copy, w2q[0], w2_raw, 0, P)
             if t == 2:
-                quantise(w2q, 0, S)
+                quantise(w2q, 0, P)
 
-        for c in range(2):
-            c0, c1 = c * HALF, (c + 1) * HALF
-            nc.scalar.copy(woven(z2q[0][:], c0, c1), planes(z2[:], c0, c1))
-        for c in range(2):
-            c0, c1 = c * HALF, (c + 1) * HALF
+        last = PACK - 1
+        rest(last)
+        first_pair = rivals(last, 0, HALF)
+        second_pair = rivals(last, HALF, S, lambda: larger(last, 0, HALF, *first_pair))
+        nc.scalar.copy(woven(z2q[0][:], 0, HALF), planes(z2[:], 0, HALF))
+        larger(last, HALF, S, *second_pair)
+        nc.scalar.copy(woven(z2q[0][:], HALF, S), planes(z2[:], HALF, S))
+        def gated(c0, c1):
             nc.vector.tensor_tensor(woven(zq[0][:], c0, c1), planes(gate[:], c0, c1), planes(st[:], c0, c1), ALU.mult)
-        for c in range(2):
-            c0, c1 = c * HALF, (c + 1) * HALF
-            quantise(zq, c0, c1)
-            quantise(z2q, c0, c1)
 
-        acc_h = [[psum.tile([P, HALF], F32, name="acc") for c in range(2)] for t in range(PACK)]
-        for c in range(2):
+        gated(0, HALF)
+        quantise(z2q, 0, HALF)
+        quantise(zq, 0, HALF)
+        gated(HALF, S)
+        quantise(z2q, HALF, S)
+        quantise(zq, HALF, S)
+
+        w3_later = (w3q[0], keep.tile([P, S], U32, name="z2_bf", align_bytes=64), w3q[2])
+        w2_later = (w2q[0], keep.tile([P, S], U32, name="z_bf", align_bytes=64), w2q[2])
+        for c0, c1 in ((P, 2 * P), (2 * P, S)):
+            quantise(w3_later, c0, c1)
+            quantise(w2_later, c0, c1)
+
+        cuts = [[(0, HALF), (HALF, S)]] + [[(0, S)]] * 3
+        acc_h = [[psum.tile([P, c1 - c0], F32, name="acc") for c0, c1 in cuts[t]] for t in range(PACK)]
+        for last_piece in (False, True):
             for t in range(PACK):
-                product(acc_h[t][c][:], w2q, t, zq[1], zq[2], c * HALF, (c + 1) * HALF, True, False)
-                product(acc_h[t][c][:], w3q, t, z2q[1], z2q[2], c * HALF, (c + 1) * HALF, False, True)
+                for acc, (c0, c1) in zip(acc_h[t], cuts[t]):
+                    if (c1 == S) == last_piece:
+                        passes = [(w3q, z2q), (w2q, zq)] if t == 0 else [(w3_later, z2q), (w2_later, zq)]
+                        for n, (w, act) in enumerate(passes):
+                            product(acc[:], w, t, act[1][:, c0:c1], act[2][:, c0:c1], n == 0, n == 1)
 
         out_rows = out.rearrange("(p t) u -> p t u", t=PACK)
 
         def leave(t):
-            for c in range(2):
-                nc.scalar.activation(r_win[t][:, c * HALF : (c + 1) * HALF], acc_h[t][c][:], ACT.Relu)
-            for c in range(2):
-                nc.scalar.copy(h_plain[t][:, c * HALF : (c + 1) * HALF], acc_h[t][c][:])
+            for acc, (c0, c1) in zip(acc_h[t], cuts[t]):
+                nc.scalar.activation(r_win[t][:, c0:c1], acc[:], ACT.Relu)
+            for acc, (c0, c1) in zip(acc_h[t], cuts[t]):
+                nc.scalar.copy(h_plain[t][:, c0:c1], acc[:])
 
         def fetch(t):
             minus = ring.tile([P, S], F32, name="minus")

@@ -71,10 +71,10 @@ def tile_picked_joinhopptrimpagez_none_p_kernel(tc, x_words, x_scales, w1, gn, g
             )
 
         def woven(ap, c0, c1):
-            return ap.rearrange("p (c i t) -> p c t i", i=4, t=PACK)[:, c0 // 4 : c1 // 4]
+            return ap.rearrange("p (c i t) -> p c t i", i=2, t=PACK)[:, c0 // 2 : c1 // 2]
 
         def planes(ap, c0, c1):
-            return ap.rearrange("p t (c i) -> p c t i", i=4)[:, c0 // 4 : c1 // 4]
+            return ap.rearrange("p t (c i) -> p c t i", i=2)[:, c0 // 2 : c1 // 2]
 
         xs = keep.tile([P, T], U8, name="xs", align_bytes=64)
         nc.gpsimd.memset(xs[:].bitcast(I32), 0)
@@ -105,49 +105,59 @@ def tile_picked_joinhopptrimpagez_none_p_kernel(tc, x_words, x_scales, w1, gn, g
         page = [keep.tile([P, U], F32, name="page%d" % t) for t in range(2)]
 
         nc.gpsimd.memset(y_win[0][:, S:], 0.0)
-        warm = keep.tile([P, 1], F32, name="warm")
-        nc.scalar.activation(warm[:], y_win[0][:, S : S + 1], ACT.Sigmoid)
         w1q = mx_tiles("w1", "xs")
-        deal_weight(nc.vector.tensor_copy, w1q[0], w1_raw, 0, 40)
-        deal_weight(nc.scalar.copy, w1q[0], w1_raw, 40, 128)
+        deal_weight(nc.vector.tensor_copy, w1q[0], w1_raw, 0, 32)
+        deal_weight(nc.scalar.copy, w1q[0], w1_raw, 32, 128)
         xg_scales = keep.tile([P, S], U8, name="xg_scales", align_bytes=64)
         nc.vector.tensor_copy(xg_scales[:], xs[:].indirect(l_offs[:]))
-        quantise(w1q, 0, S)
+        quantise(w1q, 0, P)
 
-        xg = [keep.tile([P, HALF], U32, name=name, align_bytes=64) for name in ("w1_bf", "xg1")]
+        xg = [keep.tile([P, HALF], U32, name=name, align_bytes=64) for name in ("xg0", "xg1")]
         for c in range(2):
             nc.vector.tensor_copy(xg[c][:], xw[:].bitcast(U32).indirect(l_offs[:, c * COLS : (c + 1) * COLS]))
 
         for t in range(2):
             nc.gpsimd.memset(page[t][:], 0.0)
 
+        w1_later = (w1q[0], keep.tile([P, S], U32, name="xw", align_bytes=64), w1q[2])
+        quantise(w1_later, P, 2 * P)
+        quantise(w1_later, 2 * P, S)
         gn2 = keep.tile([P, PACK], F32, name="gn2")
-        gn_neg = keep.tile([P, PACK], F32, name="gn_neg")
         gm_neg = keep.tile([P, PACK], F32, name="gm_neg")
 
         for c in range(2):
             cols = slice(c * HALF, (c + 1) * HALF)
             acc = psum.tile([P, HALF], F32, name="acc")
             product(acc[:], w1q, 0, xg[c][:], xg_scales[:, cols], True, True)
-            nc.scalar.copy(y_win[0][:, cols], acc[:])
+            if c == 0:
+                nc.scalar.copy(y_win[0][:, cols], acc[:])
+            else:
+                nc.vector.tensor_copy(y_win[0][:, cols], acc[:])
             nc.scalar.copy(y_plain[0][:, cols], acc[:])
         for t in range(1, PACK):
             acc = psum.tile([P, S], F32, name="acc")
             for c in range(2):
                 cols = slice(c * HALF, (c + 1) * HALF)
-                product(acc[:, cols], w1q, t, xg[c][:], xg_scales[:, cols], True, True)
+                product(acc[:, cols], w1_later, t, xg[c][:], xg_scales[:, cols], True, True)
             nc.scalar.copy(y_win[t][:, :S], acc[:])
             nc.scalar.copy(y_plain[t], acc[:])
 
-        for name in ("xw", "xg1"):
+        for name in ("w1_bf", "xw"):
             late = keep.tile([P, U], F32, name=name, align_bytes=64)
             nc.gpsimd.memset(late[:], 0.0)
             page.append(late)
-        nc.scalar.activation(gn2[:], gn_t[:], ACT.Copy, scale=2.0)
-        nc.scalar.activation(gn_neg[:], gn_t[:], ACT.Copy, scale=-1.0)
+        nc.scalar.activation(gn2[:], gn_t[:], ACT.Copy, scale=-2.0)
         nc.scalar.activation(gm_neg[:], gm_t[:], ACT.Copy, scale=-1.0)
-        w2q = mx_tiles("w2")
-        w3q = mx_tiles("w3")
+        w_bf = keep.tile([P, 2 * PACK * S], BF16, name="w_bf", align_bytes=64)
+        w_first = keep.tile([P, 2 * P], U32, name="w_first", align_bytes=64)
+        w_scales = keep.tile([P, 2 * S], U8, name="w_scales", align_bytes=64)
+
+        def deal_pair(which, raw):
+            nc.scalar.copy(
+                w_bf[:].rearrange("p (t w m j) -> p w m j t", t=PACK, w=2, j=PACK)[:, which],
+                raw[:].rearrange("p j (m t) -> p m j t", t=PACK),
+            )
+
         zq = mx_tiles("z")
         z2q = mx_tiles("z2")
         gate = keep.tile([P, PACK, S], F32, name="gate")
@@ -160,8 +170,8 @@ def tile_picked_joinhopptrimpagez_none_p_kernel(tc, x_words, x_scales, w1, gn, g
         def rest(t):
             nc.vector.tensor_tensor(s_win[t][:, :S], y_win[t][:].indirect(l1[:]), y_plain[t], ALU.add)
             sig = ring.tile([P, S], F32, name="sig")
-            nc.scalar.activation(sig[:], s_win[t][:].indirect(l2[:]), ACT.Sigmoid, scale=2.0)
-            nc.scalar.activation(gate[:, t, :], sig[:], ACT.Identity, scale=gn2[:, t : t + 1], bias=gn_neg[:, t : t + 1])
+            nc.scalar.activation(sig[:], s_win[t][:].indirect(l2[:]), ACT.Sigmoid, scale=-2.0)
+            nc.scalar.activation(gate[:, t, :], sig[:], ACT.Identity, scale=gn2[:, t : t + 1], bias=gn_t[:, t : t + 1])
             nc.sync.dma_start(st[:, t, :], s_win[t][:, :S])
 
         def rivals(t, c0, c1, between=None):
@@ -186,12 +196,11 @@ def tile_picked_joinhopptrimpagez_none_p_kernel(tc, x_words, x_scales, w1, gn, g
             near(t + 1)
             larger(t, 0, S, *pair)
             if t == 0:
-                deal_weight(nc.scalar.copy, w3q[0], w3_raw, 0, P)
+                deal_pair(0, w3_raw)
             if t == 1:
-                quantise(w3q, 0, P)
-                deal_weight(nc.scalar.copy, w2q[0], w2_raw, 0, P)
+                deal_pair(1, w2_raw)
             if t == 2:
-                quantise(w2q, 0, P)
+                quantise((w_bf, w_first, w_scales), 0, 2 * P)
 
         last = PACK - 1
         rest(last)
@@ -208,45 +217,57 @@ def tile_picked_joinhopptrimpagez_none_p_kernel(tc, x_words, x_scales, w1, gn, g
         quantise(zq, 0, HALF)
         gated(HALF, S)
         quantise(z2q, HALF, S)
-        quantise(zq, HALF, S)
+        z_second = (zq[0], keep.tile([P, S], U32, name="z2_bf", align_bytes=64), zq[2])
+        quantise(z_second, HALF, S)
 
-        w3_later = (w3q[0], keep.tile([P, S], U32, name="z2_bf", align_bytes=64), w3q[2])
-        w2_later = (w2q[0], keep.tile([P, S], U32, name="z_bf", align_bytes=64), w2q[2])
-        for c0, c1 in ((P, 2 * P), (2 * P, S)):
-            quantise(w3_later, c0, c1)
-            quantise(w2_later, c0, c1)
+        later_codes = keep.tile([P, 2 * S], U32, name="z_bf", align_bytes=64)
+        quantise((w_bf, later_codes, w_scales), 2 * P, S)
+        quantise((w_bf, later_codes, w_scales), S, 2 * S)
 
         cuts = [[(0, HALF), (HALF, S)]] + [[(0, S)]] * 3
         acc_h = [[psum.tile([P, c1 - c0], F32, name="acc") for c0, c1 in cuts[t]] for t in range(PACK)]
-        for last_piece in (False, True):
-            for t in range(PACK):
-                for acc, (c0, c1) in zip(acc_h[t], cuts[t]):
-                    if (c1 == S) == last_piece:
-                        passes = [(w3q, z2q), (w2q, zq)] if t == 0 else [(w3_later, z2q), (w2_later, zq)]
-                        for n, (w, act) in enumerate(passes):
-                            product(acc[:], w, t, act[1][:, c0:c1], act[2][:, c0:c1], n == 0, n == 1)
+        for t in range(PACK):
+            for c in range(2):
+                cols = slice(c * HALF, (c + 1) * HALF)
+                acc = acc_h[0][c][:] if t == 0 else acc_h[t][0][:, cols]
+                z_half = z_second if c else zq
+                w = (w_bf, later_codes if t else w_first, w_scales)
+                product(acc, w, 2 * t, z2q[1][:, cols], z2q[2][:, cols], True, False)
+                product(acc, w, 2 * t + 1, z_half[1][:, cols], z_half[2][:, cols], False, True)
 
         out_rows = out.rearrange("(p t) u -> p t u", t=PACK)
 
         def leave(t):
             for acc, (c0, c1) in zip(acc_h[t], cuts[t]):
-                nc.scalar.activation(r_win[t][:, c0:c1], acc[:], ACT.Relu)
+                if t == 0:
+                    nc.scalar.activation(r_win[t][:, c0:c1], acc[:], ACT.Relu)
+                else:
+                    pos = ring.tile([P, S], F32, name="pos")
+                    nc.scalar.activation(pos[:], acc[:], ACT.Relu)
+                    nc.scalar.activation(r_win[t][:, c0:c1], pos[:], ACT.Copy, scale=-1.0)
             for acc, (c0, c1) in zip(acc_h[t], cuts[t]):
                 nc.scalar.copy(h_plain[t][:, c0:c1], acc[:])
 
         def fetch(t):
             minus = ring.tile([P, S], F32, name="minus")
-            nc.vector.tensor_scalar(minus[:], r_win[t][:].indirect(l7[:]), -1.0, 0.0, ALU.mult, ALU.add)
+            if t == 0:
+                nc.vector.tensor_scalar(minus[:], r_win[t][:].indirect(l7[:]), -1.0, 0.0, ALU.mult, ALU.add)
+            else:
+                nc.vector.tensor_tensor(minus[:], r_win[t][:].indirect(l7[:]), h_plain[t], ALU.add)
             return minus
 
         def put(t, minus):
-            nc.vector.tensor_tensor(page[t][:].indirect(l6[:]), h_plain[t], minus[:], ALU.add)
+            if t == 0:
+                nc.vector.tensor_tensor(page[t][:].indirect(l6[:]), h_plain[t], minus[:], ALU.add)
+            else:
+                nc.vector.tensor_copy(page[t][:].indirect(l6[:]), minus[:])
             nc.sync.dma_start(out_rows[:, t, :], page[t][:])
 
         for t in range(PACK):
             leave(t)
-        minus = fetch(0)
-        for t in range(PACK):
+        put(0, fetch(0))
+        minus = fetch(1)
+        for t in range(1, PACK):
             ahead = fetch(t + 1) if t + 1 < PACK else None
             put(t, minus)
             minus = ahead

@@ -17,8 +17,12 @@ ACT = mybir.ActivationFunctionType
 
 P = 128
 PACK = 4
+LAST = PACK - 1
+STRIPE = 16
 HALF = S // 2
-COLS = HALF // 16
+HALVES = ((0, HALF), (HALF, S))
+QUADRANT = 32
+W1_ON_VECTOR = 32
 
 
 def tile_picked_joinhopptrimpagez_none_p_kernel(tc, x_words, x_scales, w1, gn, gm, w2, w3, offs, n1, n2, n3, n4, n5, n6, n7, out):
@@ -29,60 +33,54 @@ def tile_picked_joinhopptrimpagez_none_p_kernel(tc, x_words, x_scales, w1, gn, g
         psum = ctx.enter_context(tc.psum_pool(name="psum", bufs=8))
 
         def load_list(src, name):
-            t = keep.tile([P, S // 16], U16, name=name)
-            nc.sync.dma_start(t[:], src)
-            return t
+            entries = keep.tile([P, S // STRIPE], U16, name=name)
+            nc.sync.dma_start(entries[:], src)
+            return entries
 
         def load_weight(src, name):
-            t = keep.tile([P, PACK, H], F32, name=name)
-            nc.sync.dma_start(t[:], src.rearrange("(p j) c -> p j c", j=PACK))
-            return t
+            raw = keep.tile([P, PACK, H], F32, name=name)
+            nc.sync.dma_start(raw[:], src.rearrange("(p j) c -> p j c", j=PACK))
+            return raw
 
         def load_gain(src, name):
-            t = keep.tile([P, PACK], F32, name=name)
-            nc.sync.dma_start(t[:], src.rearrange("(p t) o -> p (t o)", t=PACK))
-            return t
+            gain = keep.tile([P, PACK], F32, name=name)
+            nc.sync.dma_start(gain[:], src.rearrange("(p t) o -> p (t o)", t=PACK))
+            return gain
 
-        def deal_weight(copy, grouped, raw, m0, m1):
-            copy(
-                grouped[:].rearrange("p (t m j) -> p m j t", t=PACK, j=PACK)[:, m0:m1],
-                raw[:].rearrange("p j (m t) -> p m j t", t=PACK)[:, m0:m1],
-            )
+        def quads(raw):
+            return raw[:].rearrange("p j (m t) -> p m j t", t=PACK)
 
-        def mx_tiles(name, scales_tag=None):
-            grouped = keep.tile([P, PACK * S], BF16, name=name + "_bf", align_bytes=64)
-            codes = keep.tile([P, S], U32, name=name + "_codes", align_bytes=64)
-            scales = keep.tile([P, S], U8, name=scales_tag or name + "_scales", align_bytes=64)
-            return grouped, codes, scales
+        def quantise(rounded, codes, scales, c0, c1):
+            nc.vector.quantize_mx(out=codes[:, c0:c1].bitcast(FP8X4), scales=scales[:, c0:c1], in_=rounded[:, PACK * c0 : PACK * c1])
 
-        def quantise(tiles, c0, c1):
-            grouped, codes, scales = tiles
-            nc.vector.quantize_mx(out=codes[:, c0:c1].bitcast(FP8X4), scales=scales[:, c0:c1], in_=grouped[:, PACK * c0 : PACK * c1])
-
-        def product(acc, w, t, codes, scales, start, stop):
+        def product(acc, w_codes, w_scales, block, codes, scales, start, stop):
             nc.tensor.matmul_mx(
                 out=acc,
-                lhsT=w[1][:, t * P : (t + 1) * P].bitcast(FP8X4),
-                lhsT_scale=w[2][:, t * P : (t + 1) * P],
+                lhsT=w_codes[:, block * P : (block + 1) * P].bitcast(FP8X4),
+                lhsT_scale=w_scales[:, block * P : (block + 1) * P],
                 rhs=codes.bitcast(FP8X4),
                 rhs_scale=scales,
                 start=start,
                 stop=stop,
             )
 
-        def woven(ap, c0, c1):
-            return ap.rearrange("p (c i t) -> p c t i", i=2, t=PACK)[:, c0 // 2 : c1 // 2]
+        def woven(rounded, c0, c1):
+            return rounded[:].rearrange("p (c i t) -> p c t i", i=2, t=PACK)[:, c0 // 2 : c1 // 2]
 
-        def planes(ap, c0, c1):
-            return ap.rearrange("p t (c i) -> p c t i", i=2)[:, c0 // 2 : c1 // 2]
+        def by_tile(tiles, c0, c1):
+            return tiles[:].rearrange("p t (c i) -> p c t i", i=2)[:, c0 // 2 : c1 // 2]
+
+        def entries(lists, c0, c1):
+            return lists[:, c0 // STRIPE : c1 // STRIPE]
 
         xs = keep.tile([P, T], U8, name="xs", align_bytes=64)
         nc.gpsimd.memset(xs[:].bitcast(I32), 0)
         w1_raw = load_weight(w1, "w1_raw")
         l_offs = load_list(offs, "offs")
         l3 = load_list(n3, "n3")
-        for q in range(4):
-            nc.sync.dma_start(xs[32 * q : 32 * q + 4, :].bitcast(I32), x_scales[0, 4 * q : 4 * q + 4, :].bitcast(I32))
+        for q in range(P // QUADRANT):
+            rows = x_scales[0, PACK * q : PACK * (q + 1), :]
+            nc.sync.dma_start(xs[QUADRANT * q : QUADRANT * q + PACK, :].bitcast(I32), rows.bitcast(I32))
         xw = keep.tile([P, T], I32, name="xw", align_bytes=64)
         nc.sync.dma_start(xw[:], x_words[0].rearrange("p c r -> p (c r)").bitcast(I32))
         l1 = load_list(n1, "n1")
@@ -96,178 +94,165 @@ def tile_picked_joinhopptrimpagez_none_p_kernel(tc, x_words, x_scales, w1, gn, g
         l7 = load_list(n7, "n7")
         l6 = load_list(n6, "n6")
 
-        y_win = [keep.tile([P, 2 * S], F32, name="y_win%d" % t) for t in range(PACK)]
-        y_last = keep.tile([P, S], F32, name="y_last")
-        y_plain = [y_win[t + 1][:, S:] for t in range(PACK - 1)] + [y_last[:]]
-        r_win = y_win
-        h_plain = y_plain
-        s_win = [keep.tile([P, 2 * S], F32, name="s_win%d" % t) for t in range(PACK)]
+        window = [keep.tile([P, 2 * S], F32, name="window%d" % t) for t in range(PACK)]
+        plain_last = keep.tile([P, S], F32, name="plain_last")
+        plain = [window[t + 1][:, S:] for t in range(LAST)] + [plain_last[:]]
+        st_window = [keep.tile([P, 2 * S], F32, name="st_window%d" % t) for t in range(PACK)]
         page = [keep.tile([P, U], F32, name="page%d" % t) for t in range(2)]
+        nc.gpsimd.memset(window[0][:, S:], 0.0)
 
-        nc.gpsimd.memset(y_win[0][:, S:], 0.0)
-        w1q = mx_tiles("w1", "xs")
-        deal_weight(nc.vector.tensor_copy, w1q[0], w1_raw, 0, 32)
-        deal_weight(nc.scalar.copy, w1q[0], w1_raw, 32, 128)
+        w1_bf = keep.tile([P, PACK * H], BF16, name="w1_bf", align_bytes=64)
+        w1_first = keep.tile([P, H], U32, name="w1_first", align_bytes=64)
+        w1_scales = keep.tile([P, H], U8, name="xs", align_bytes=64)
+        w1_dealt = w1_bf[:].rearrange("p (t m j) -> p m j t", t=PACK, j=PACK)
+        nc.vector.tensor_copy(w1_dealt[:, :W1_ON_VECTOR], quads(w1_raw)[:, :W1_ON_VECTOR])
+        nc.scalar.copy(w1_dealt[:, W1_ON_VECTOR:], quads(w1_raw)[:, W1_ON_VECTOR:])
         xg_scales = keep.tile([P, S], U8, name="xg_scales", align_bytes=64)
         nc.vector.tensor_copy(xg_scales[:], xs[:].indirect(l_offs[:]))
-        quantise(w1q, 0, P)
+        quantise(w1_bf, w1_first, w1_scales, 0, P)
 
-        xg = [keep.tile([P, HALF], U32, name=name, align_bytes=64) for name in ("xg0", "xg1")]
-        for c in range(2):
-            nc.vector.tensor_copy(xg[c][:], xw[:].bitcast(U32).indirect(l_offs[:, c * COLS : (c + 1) * COLS]))
+        xg = [keep.tile([P, HALF], U32, name="xg%d" % c, align_bytes=64) for c in range(2)]
+        for c, (c0, c1) in enumerate(HALVES):
+            nc.vector.tensor_copy(xg[c][:], xw[:].bitcast(U32).indirect(entries(l_offs, c0, c1)))
 
         for t in range(2):
             nc.gpsimd.memset(page[t][:], 0.0)
 
-        w1_later = (w1q[0], keep.tile([P, S], U32, name="xw", align_bytes=64), w1q[2])
-        quantise(w1_later, P, 2 * P)
-        quantise(w1_later, 2 * P, S)
-        gn2 = keep.tile([P, PACK], F32, name="gn2")
+        w1_later = keep.tile([P, H], U32, name="xw", align_bytes=64)
+        quantise(w1_bf, w1_later, w1_scales, P, 2 * P)
+        quantise(w1_bf, w1_later, w1_scales, 2 * P, H)
+        gn_scale = keep.tile([P, PACK], F32, name="gn_scale")
         gm_neg = keep.tile([P, PACK], F32, name="gm_neg")
 
-        for c in range(2):
-            cols = slice(c * HALF, (c + 1) * HALF)
+        for c, (c0, c1) in enumerate(HALVES):
             acc = psum.tile([P, HALF], F32, name="acc")
-            product(acc[:], w1q, 0, xg[c][:], xg_scales[:, cols], True, True)
-            if c == 0:
-                nc.scalar.copy(y_win[0][:, cols], acc[:])
-            else:
-                nc.vector.tensor_copy(y_win[0][:, cols], acc[:])
-            nc.scalar.copy(y_plain[0][:, cols], acc[:])
+            product(acc[:], w1_first, w1_scales, 0, xg[c][:], xg_scales[:, c0:c1], True, True)
+            empty = nc.vector.tensor_copy if c else nc.scalar.copy
+            empty(window[0][:, c0:c1], acc[:])
+            nc.scalar.copy(plain[0][:, c0:c1], acc[:])
         for t in range(1, PACK):
             acc = psum.tile([P, S], F32, name="acc")
-            for c in range(2):
-                cols = slice(c * HALF, (c + 1) * HALF)
-                product(acc[:, cols], w1_later, t, xg[c][:], xg_scales[:, cols], True, True)
-            nc.scalar.copy(y_win[t][:, :S], acc[:])
-            nc.scalar.copy(y_plain[t], acc[:])
+            for c, (c0, c1) in enumerate(HALVES):
+                product(acc[:, c0:c1], w1_later, w1_scales, t, xg[c][:], xg_scales[:, c0:c1], True, True)
+            nc.scalar.copy(window[t][:, :S], acc[:])
+            nc.scalar.copy(plain[t], acc[:])
 
         for name in ("w1_bf", "xw"):
-            late = keep.tile([P, U], F32, name=name, align_bytes=64)
-            nc.gpsimd.memset(late[:], 0.0)
-            page.append(late)
-        nc.scalar.activation(gn2[:], gn_t[:], ACT.Copy, scale=-2.0)
+            late_page = keep.tile([P, U], F32, name=name, align_bytes=64)
+            nc.gpsimd.memset(late_page[:], 0.0)
+            page.append(late_page)
+        nc.scalar.activation(gn_scale[:], gn_t[:], ACT.Copy, scale=-2.0)
         nc.scalar.activation(gm_neg[:], gm_t[:], ACT.Copy, scale=-1.0)
-        w_bf = keep.tile([P, 2 * PACK * S], BF16, name="w_bf", align_bytes=64)
-        w_first = keep.tile([P, 2 * P], U32, name="w_first", align_bytes=64)
-        w_scales = keep.tile([P, 2 * S], U8, name="w_scales", align_bytes=64)
 
-        def deal_pair(which, raw):
-            nc.scalar.copy(
-                w_bf[:].rearrange("p (t w m j) -> p w m j t", t=PACK, w=2, j=PACK)[:, which],
-                raw[:].rearrange("p j (m t) -> p m j t", t=PACK),
-            )
+        w23_bf = keep.tile([P, 2 * PACK * N], BF16, name="w23_bf", align_bytes=64)
+        w23_first = keep.tile([P, 2 * P], U32, name="w23_first", align_bytes=64)
+        w23_scales = keep.tile([P, 2 * N], U8, name="w23_scales", align_bytes=64)
+        w23_dealt = w23_bf[:].rearrange("p (t w m j) -> p w m j t", t=PACK, w=2, j=PACK)
 
-        zq = mx_tiles("z")
-        z2q = mx_tiles("z2")
+        z_bf = keep.tile([P, PACK * S], BF16, name="z_bf", align_bytes=64)
+        z_first = keep.tile([P, S], U32, name="z_first", align_bytes=64)
+        z_scales = keep.tile([P, S], U8, name="z_scales", align_bytes=64)
+        z2_bf = keep.tile([P, PACK * S], BF16, name="z2_bf", align_bytes=64)
+        z2_codes = keep.tile([P, S], U32, name="z2_codes", align_bytes=64)
+        z2_scales = keep.tile([P, S], U8, name="z2_scales", align_bytes=64)
         gate = keep.tile([P, PACK, S], F32, name="gate")
         st = keep.tile([P, PACK, S], F32, name="st")
         z2 = keep.tile([P, PACK, S], F32, name="z2")
 
-        def near(t, c0=0, c1=S):
-            nc.vector.tensor_tensor(s_win[t][:, S + c0 : S + c1], y_win[t][:].indirect(l3[:, c0 // 16 : c1 // 16]), y_plain[t][:, c0:c1], ALU.add)
+        def pair_sum(t, c0, c1):
+            nc.vector.tensor_tensor(st_window[t][:, S + c0 : S + c1], window[t][:].indirect(entries(l3, c0, c1)), plain[t][:, c0:c1], ALU.add)
 
-        def rest(t):
-            nc.vector.tensor_tensor(s_win[t][:, :S], y_win[t][:].indirect(l1[:]), y_plain[t], ALU.add)
+        def st_and_gate(t):
+            nc.vector.tensor_tensor(st_window[t][:, :S], window[t][:].indirect(l1[:]), plain[t], ALU.add)
             sig = ring.tile([P, S], F32, name="sig")
-            nc.scalar.activation(sig[:], s_win[t][:].indirect(l2[:]), ACT.Sigmoid, scale=-2.0)
-            nc.scalar.activation(gate[:, t, :], sig[:], ACT.Identity, scale=gn2[:, t : t + 1], bias=gn_t[:, t : t + 1])
-            nc.sync.dma_start(st[:, t, :], s_win[t][:, :S])
+            nc.scalar.activation(sig[:], st_window[t][:].indirect(l2[:]), ACT.Sigmoid, scale=-2.0)
+            nc.scalar.activation(gate[:, t, :], sig[:], ACT.Identity, scale=gn_scale[:, t : t + 1], bias=gn_t[:, t : t + 1])
+            nc.sync.dma_start(st[:, t, :], st_window[t][:, :S])
 
-        def rivals(t, c0, c1, between=None):
-            q4 = ring.tile([P, c1 - c0], F32, name="q4")
-            q5 = ring.tile([P, c1 - c0], F32, name="q5")
-            nc.vector.tensor_tensor(q4[:], y_win[t][:].indirect(l4[:, c0 // 16 : c1 // 16]), s_win[t][:, S + c0 : S + c1], ALU.subtract)
-            if between:
-                between()
-            nc.vector.tensor_tensor(q5[:], y_win[t][:].indirect(l5[:, c0 // 16 : c1 // 16]), s_win[t][:, S + c0 : S + c1], ALU.subtract)
-            return q4, q5
+        def rival(t, lists, name, c0, c1):
+            less = ring.tile([P, c1 - c0], F32, name=name)
+            nc.vector.tensor_tensor(less[:], window[t][:].indirect(entries(lists, c0, c1)), st_window[t][:, S + c0 : S + c1], ALU.subtract)
+            return less
 
-        def larger(t, c0, c1, q4, q5):
-            big = ring.tile([P, c1 - c0], F32, name="big")
-            nc.vector.tensor_tensor(big[:], q4[:], q5[:], ALU.max)
-            nc.scalar.activation(z2[:, t, c0:c1], big[:], ACT.Copy, scale=gm_neg[:, t : t + 1])
+        def z2_rows(t, c0, c1, less4, less5):
+            larger = ring.tile([P, c1 - c0], F32, name="larger")
+            nc.vector.tensor_tensor(larger[:], less4[:], less5[:], ALU.max)
+            nc.scalar.activation(z2[:, t, c0:c1], larger[:], ACT.Copy, scale=gm_neg[:, t : t + 1])
 
-        near(0, 0, HALF)
-        near(0, HALF, S)
-        for t in range(PACK - 1):
-            rest(t)
-            pair = rivals(t, 0, S)
-            near(t + 1)
-            larger(t, 0, S, *pair)
-            if t == 0:
-                deal_pair(0, w3_raw)
-            if t == 1:
-                deal_pair(1, w2_raw)
-            if t == 2:
-                quantise((w_bf, w_first, w_scales), 0, 2 * P)
+        def round_z2(c0, c1):
+            nc.scalar.copy(woven(z2_bf, c0, c1), by_tile(z2, c0, c1))
 
-        last = PACK - 1
-        rest(last)
-        first_pair = rivals(last, 0, HALF)
-        second_pair = rivals(last, HALF, S, lambda: larger(last, 0, HALF, *first_pair))
-        nc.scalar.copy(woven(z2q[0][:], 0, HALF), planes(z2[:], 0, HALF))
-        larger(last, HALF, S, *second_pair)
-        nc.scalar.copy(woven(z2q[0][:], HALF, S), planes(z2[:], HALF, S))
-        def gated(c0, c1):
-            nc.vector.tensor_tensor(woven(zq[0][:], c0, c1), planes(gate[:], c0, c1), planes(st[:], c0, c1), ALU.mult)
+        def round_z(c0, c1):
+            nc.vector.tensor_tensor(woven(z_bf, c0, c1), by_tile(gate, c0, c1), by_tile(st, c0, c1), ALU.mult)
 
-        gated(0, HALF)
-        quantise(z2q, 0, HALF)
-        quantise(zq, 0, HALF)
-        gated(HALF, S)
-        quantise(z2q, HALF, S)
-        z_second = (zq[0], keep.tile([P, S], U32, name="z2_bf", align_bytes=64), zq[2])
-        quantise(z_second, HALF, S)
+        weight_steps = (
+            lambda: nc.scalar.copy(w23_dealt[:, 0], quads(w3_raw)),
+            lambda: nc.scalar.copy(w23_dealt[:, 1], quads(w2_raw)),
+            lambda: quantise(w23_bf, w23_first, w23_scales, 0, 2 * P),
+        )
+        for c0, c1 in HALVES:
+            pair_sum(0, c0, c1)
+        for t in range(LAST):
+            st_and_gate(t)
+            less4 = rival(t, l4, "less4", 0, S)
+            less5 = rival(t, l5, "less5", 0, S)
+            pair_sum(t + 1, 0, S)
+            z2_rows(t, 0, S, less4, less5)
+            weight_steps[t]()
 
-        later_codes = keep.tile([P, 2 * S], U32, name="z_bf", align_bytes=64)
-        quantise((w_bf, later_codes, w_scales), 2 * P, S)
-        quantise((w_bf, later_codes, w_scales), S, 2 * S)
+        st_and_gate(LAST)
+        first4 = rival(LAST, l4, "less4", 0, HALF)
+        first5 = rival(LAST, l5, "less5", 0, HALF)
+        second4 = rival(LAST, l4, "less4", HALF, S)
+        z2_rows(LAST, 0, HALF, first4, first5)
+        second5 = rival(LAST, l5, "less5", HALF, S)
+        round_z2(0, HALF)
+        z2_rows(LAST, HALF, S, second4, second5)
+        round_z2(HALF, S)
 
-        cuts = [[(0, HALF), (HALF, S)]] + [[(0, S)]] * 3
-        acc_h = [[psum.tile([P, c1 - c0], F32, name="acc") for c0, c1 in cuts[t]] for t in range(PACK)]
+        round_z(0, HALF)
+        quantise(z2_bf, z2_codes, z2_scales, 0, HALF)
+        quantise(z_bf, z_first, z_scales, 0, HALF)
+        round_z(HALF, S)
+        quantise(z2_bf, z2_codes, z2_scales, HALF, S)
+        z_second = keep.tile([P, S], U32, name="z2_bf", align_bytes=64)
+        quantise(z_bf, z_second, z_scales, HALF, S)
+
+        w23_later = keep.tile([P, 2 * N], U32, name="z_bf", align_bytes=64)
+        quantise(w23_bf, w23_later, w23_scales, 2 * P, N)
+        quantise(w23_bf, w23_later, w23_scales, N, 2 * N)
+
+        pieces = [HALVES] + [((0, S),)] * LAST
+        acc_h = [[psum.tile([P, c1 - c0], F32, name="acc") for c0, c1 in pieces[t]] for t in range(PACK)]
         for t in range(PACK):
-            for c in range(2):
-                cols = slice(c * HALF, (c + 1) * HALF)
-                acc = acc_h[0][c][:] if t == 0 else acc_h[t][0][:, cols]
-                z_half = z_second if c else zq
-                w = (w_bf, later_codes if t else w_first, w_scales)
-                product(acc, w, 2 * t, z2q[1][:, cols], z2q[2][:, cols], True, False)
-                product(acc, w, 2 * t + 1, z_half[1][:, cols], z_half[2][:, cols], False, True)
+            w_codes = w23_later if t else w23_first
+            for c, (c0, c1) in enumerate(HALVES):
+                acc = acc_h[t][0][:, c0:c1] if t else acc_h[0][c][:]
+                z_codes = z_second if c else z_first
+                product(acc, w_codes, w23_scales, 2 * t, z2_codes[:, c0:c1], z2_scales[:, c0:c1], True, False)
+                product(acc, w_codes, w23_scales, 2 * t + 1, z_codes[:, c0:c1], z_scales[:, c0:c1], False, True)
+
+        for t in range(PACK):
+            for acc, (c0, c1) in zip(acc_h[t], pieces[t]):
+                nc.scalar.activation(window[t][:, c0:c1], acc[:], ACT.Relu)
+            for acc, (c0, c1) in zip(acc_h[t], pieces[t]):
+                nc.scalar.copy(plain[t][:, c0:c1], acc[:])
 
         out_rows = out.rearrange("(p t) u -> p t u", t=PACK)
 
-        def leave(t):
-            for acc, (c0, c1) in zip(acc_h[t], cuts[t]):
-                if t == 0:
-                    nc.scalar.activation(r_win[t][:, c0:c1], acc[:], ACT.Relu)
-                else:
-                    pos = ring.tile([P, S], F32, name="pos")
-                    nc.scalar.activation(pos[:], acc[:], ACT.Relu)
-                    nc.scalar.activation(r_win[t][:, c0:c1], pos[:], ACT.Copy, scale=-1.0)
-            for acc, (c0, c1) in zip(acc_h[t], cuts[t]):
-                nc.scalar.copy(h_plain[t][:, c0:c1], acc[:])
-
         def fetch(t):
             minus = ring.tile([P, S], F32, name="minus")
-            if t == 0:
-                nc.vector.tensor_scalar(minus[:], r_win[t][:].indirect(l7[:]), -1.0, 0.0, ALU.mult, ALU.add)
-            else:
-                nc.vector.tensor_tensor(minus[:], r_win[t][:].indirect(l7[:]), h_plain[t], ALU.add)
+            nc.vector.tensor_scalar(minus[:], window[t][:].indirect(l7[:]), -1.0, 0.0, ALU.mult, ALU.add)
             return minus
 
         def put(t, minus):
-            if t == 0:
-                nc.vector.tensor_tensor(page[t][:].indirect(l6[:]), h_plain[t], minus[:], ALU.add)
-            else:
-                nc.vector.tensor_copy(page[t][:].indirect(l6[:]), minus[:])
+            nc.vector.tensor_tensor(page[t][:].indirect(l6[:]), plain[t], minus[:], ALU.add)
             nc.sync.dma_start(out_rows[:, t, :], page[t][:])
 
-        for t in range(PACK):
-            leave(t)
         put(0, fetch(0))
         minus = fetch(1)
-        for t in range(1, PACK):
-            ahead = fetch(t + 1) if t + 1 < PACK else None
+        for t in range(1, LAST):
+            ahead = fetch(t + 1)
             put(t, minus)
             minus = ahead
+        put(LAST, minus)

from contextlib import ExitStack

import concourse.mybir as mybir

K, T, S, N, H, U = 512, 2048, 512, 512, 512, 1024
FLOPS = 2 * S * (K * H + 2 * H * N)

F32 = mybir.dt.float32
BF16 = mybir.dt.bfloat16
I32 = mybir.dt.int32
U32 = mybir.dt.uint32
U16 = mybir.dt.uint16
U8 = mybir.dt.uint8
FP8X4 = mybir.dt.float8_e4m3fn_x4
ALU = mybir.AluOpType
ACT = mybir.ActivationFunctionType

P = 128
PACK = 4
LAST = PACK - 1
STRIPE = 16
HALF = S // 2
HALVES = ((0, HALF), (HALF, S))
QUADRANT = 32
W1_ON_VECTOR = 32


def tile_picked_joinhopptrimpagez_none_p_kernel(tc, x_words, x_scales, w1, gn, gm, w2, w3, offs, n1, n2, n3, n4, n5, n6, n7, out):
    nc = tc.nc
    with ExitStack() as ctx:
        keep = ctx.enter_context(tc.tile_pool(name="keep", bufs=1))
        ring = ctx.enter_context(tc.tile_pool(name="ring", bufs=2))
        psum = ctx.enter_context(tc.psum_pool(name="psum", bufs=8))

        def load_list(src, name):
            entries = keep.tile([P, S // STRIPE], U16, name=name)
            nc.sync.dma_start(entries[:], src)
            return entries

        def load_weight(src, name):
            raw = keep.tile([P, PACK, H], F32, name=name)
            nc.sync.dma_start(raw[:], src.rearrange("(p j) c -> p j c", j=PACK))
            return raw

        def load_gain(src, name):
            gain = keep.tile([P, PACK], F32, name=name)
            nc.sync.dma_start(gain[:], src.rearrange("(p t) o -> p (t o)", t=PACK))
            return gain

        def quads(raw):
            return raw[:].rearrange("p j (m t) -> p m j t", t=PACK)

        def quantise(rounded, codes, scales, c0, c1):
            nc.vector.quantize_mx(out=codes[:, c0:c1].bitcast(FP8X4), scales=scales[:, c0:c1], in_=rounded[:, PACK * c0 : PACK * c1])

        def product(acc, w_codes, w_scales, block, codes, scales, start, stop):
            nc.tensor.matmul_mx(
                out=acc,
                lhsT=w_codes[:, block * P : (block + 1) * P].bitcast(FP8X4),
                lhsT_scale=w_scales[:, block * P : (block + 1) * P],
                rhs=codes.bitcast(FP8X4),
                rhs_scale=scales,
                start=start,
                stop=stop,
            )

        def woven(rounded, c0, c1):
            return rounded[:].rearrange("p (c i t) -> p c t i", i=2, t=PACK)[:, c0 // 2 : c1 // 2]

        def by_tile(tiles, c0, c1):
            return tiles[:].rearrange("p t (c i) -> p c t i", i=2)[:, c0 // 2 : c1 // 2]

        def entries(lists, c0, c1):
            return lists[:, c0 // STRIPE : c1 // STRIPE]

        xs = keep.tile([P, T], U8, name="xs", align_bytes=64)
        nc.gpsimd.memset(xs[:].bitcast(I32), 0)
        w1_raw = load_weight(w1, "w1_raw")
        l_offs = load_list(offs, "offs")
        l3 = load_list(n3, "n3")
        for q in range(P // QUADRANT):
            rows = x_scales[0, PACK * q : PACK * (q + 1), :]
            nc.sync.dma_start(xs[QUADRANT * q : QUADRANT * q + PACK, :].bitcast(I32), rows.bitcast(I32))
        xw = keep.tile([P, T], I32, name="xw", align_bytes=64)
        nc.sync.dma_start(xw[:], x_words[0].rearrange("p c r -> p (c r)").bitcast(I32))
        l1 = load_list(n1, "n1")
        l4 = load_list(n4, "n4")
        l5 = load_list(n5, "n5")
        l2 = load_list(n2, "n2")
        gn_t = load_gain(gn, "gn")
        gm_t = load_gain(gm, "gm")
        w3_raw = load_weight(w3, "w3_raw")
        w2_raw = load_weight(w2, "w2_raw")
        l7 = load_list(n7, "n7")
        l6 = load_list(n6, "n6")

        window = [keep.tile([P, 2 * S], F32, name="window%d" % t) for t in range(PACK)]
        plain_last = keep.tile([P, S], F32, name="plain_last")
        plain = [window[t + 1][:, S:] for t in range(LAST)] + [plain_last[:]]
        st_window = [keep.tile([P, 2 * S], F32, name="st_window%d" % t) for t in range(PACK)]
        page = [keep.tile([P, U], F32, name="page%d" % t) for t in range(2)]
        nc.gpsimd.memset(window[0][:, S:], 0.0)

        w1_bf = keep.tile([P, PACK * H], BF16, name="w1_bf", align_bytes=64)
        w1_first = keep.tile([P, H], U32, name="w1_first", align_bytes=64)
        w1_scales = keep.tile([P, H], U8, name="xs", align_bytes=64)
        w1_dealt = w1_bf[:].rearrange("p (t m j) -> p m j t", t=PACK, j=PACK)
        nc.vector.tensor_copy(w1_dealt[:, :W1_ON_VECTOR], quads(w1_raw)[:, :W1_ON_VECTOR])
        nc.scalar.copy(w1_dealt[:, W1_ON_VECTOR:], quads(w1_raw)[:, W1_ON_VECTOR:])
        xg_scales = keep.tile([P, S], U8, name="xg_scales", align_bytes=64)
        nc.vector.tensor_copy(xg_scales[:], xs[:].indirect(l_offs[:]))
        quantise(w1_bf, w1_first, w1_scales, 0, P)

        xg = [keep.tile([P, HALF], U32, name="xg%d" % c, align_bytes=64) for c in range(2)]
        for c, (c0, c1) in enumerate(HALVES):
            nc.vector.tensor_copy(xg[c][:], xw[:].bitcast(U32).indirect(entries(l_offs, c0, c1)))

        for t in range(2):
            nc.gpsimd.memset(page[t][:], 0.0)

        w1_later = keep.tile([P, H], U32, name="xw", align_bytes=64)
        quantise(w1_bf, w1_later, w1_scales, P, 2 * P)
        quantise(w1_bf, w1_later, w1_scales, 2 * P, H)
        gn_scale = keep.tile([P, PACK], F32, name="gn_scale")
        gm_neg = keep.tile([P, PACK], F32, name="gm_neg")

        for c, (c0, c1) in enumerate(HALVES):
            acc = psum.tile([P, HALF], F32, name="acc")
            product(acc[:], w1_first, w1_scales, 0, xg[c][:], xg_scales[:, c0:c1], True, True)
            empty = nc.vector.tensor_copy if c else nc.scalar.copy
            empty(window[0][:, c0:c1], acc[:])
            nc.scalar.copy(plain[0][:, c0:c1], acc[:])
        for t in range(1, PACK):
            acc = psum.tile([P, S], F32, name="acc")
            for c, (c0, c1) in enumerate(HALVES):
                product(acc[:, c0:c1], w1_later, w1_scales, t, xg[c][:], xg_scales[:, c0:c1], True, True)
            nc.scalar.copy(window[t][:, :S], acc[:])
            nc.scalar.copy(plain[t], acc[:])

        for name in ("w1_bf", "xw"):
            late_page = keep.tile([P, U], F32, name=name, align_bytes=64)
            nc.gpsimd.memset(late_page[:], 0.0)
            page.append(late_page)
        nc.scalar.activation(gn_scale[:], gn_t[:], ACT.Copy, scale=-2.0)
        nc.scalar.activation(gm_neg[:], gm_t[:], ACT.Copy, scale=-1.0)

        w23_bf = keep.tile([P, 2 * PACK * N], BF16, name="w23_bf", align_bytes=64)
        w23_first = keep.tile([P, 2 * P], U32, name="w23_first", align_bytes=64)
        w23_scales = keep.tile([P, 2 * N], U8, name="w23_scales", align_bytes=64)
        w23_dealt = w23_bf[:].rearrange("p (t w m j) -> p w m j t", t=PACK, w=2, j=PACK)

        z_bf = keep.tile([P, PACK * S], BF16, name="z_bf", align_bytes=64)
        z_first = keep.tile([P, S], U32, name="z_first", align_bytes=64)
        z_scales = keep.tile([P, S], U8, name="z_scales", align_bytes=64)
        z2_bf = keep.tile([P, PACK * S], BF16, name="z2_bf", align_bytes=64)
        z2_codes = keep.tile([P, S], U32, name="z2_codes", align_bytes=64)
        z2_scales = keep.tile([P, S], U8, name="z2_scales", align_bytes=64)
        gate = keep.tile([P, PACK, S], F32, name="gate")
        st = keep.tile([P, PACK, S], F32, name="st")
        z2 = keep.tile([P, PACK, S], F32, name="z2")

        def pair_sum(t, c0, c1):
            nc.vector.tensor_tensor(st_window[t][:, S + c0 : S + c1], window[t][:].indirect(entries(l3, c0, c1)), plain[t][:, c0:c1], ALU.add)

        def st_and_gate(t):
            nc.vector.tensor_tensor(st_window[t][:, :S], window[t][:].indirect(l1[:]), plain[t], ALU.add)
            sig = ring.tile([P, S], F32, name="sig")
            nc.scalar.activation(sig[:], st_window[t][:].indirect(l2[:]), ACT.Sigmoid, scale=-2.0)
            nc.scalar.activation(gate[:, t, :], sig[:], ACT.Identity, scale=gn_scale[:, t : t + 1], bias=gn_t[:, t : t + 1])
            nc.sync.dma_start(st[:, t, :], st_window[t][:, :S])

        def rival(t, lists, name, c0, c1):
            less = ring.tile([P, c1 - c0], F32, name=name)
            nc.vector.tensor_tensor(less[:], window[t][:].indirect(entries(lists, c0, c1)), st_window[t][:, S + c0 : S + c1], ALU.subtract)
            return less

        def z2_rows(t, c0, c1, less4, less5):
            larger = ring.tile([P, c1 - c0], F32, name="larger")
            nc.vector.tensor_tensor(larger[:], less4[:], less5[:], ALU.max)
            nc.scalar.activation(z2[:, t, c0:c1], larger[:], ACT.Copy, scale=gm_neg[:, t : t + 1])

        def round_z2(c0, c1):
            nc.scalar.copy(woven(z2_bf, c0, c1), by_tile(z2, c0, c1))

        def round_z(c0, c1):
            nc.vector.tensor_tensor(woven(z_bf, c0, c1), by_tile(gate, c0, c1), by_tile(st, c0, c1), ALU.mult)

        weight_steps = (
            lambda: nc.scalar.copy(w23_dealt[:, 0], quads(w3_raw)),
            lambda: nc.scalar.copy(w23_dealt[:, 1], quads(w2_raw)),
            lambda: quantise(w23_bf, w23_first, w23_scales, 0, 2 * P),
        )
        for c0, c1 in HALVES:
            pair_sum(0, c0, c1)
        for t in range(LAST):
            st_and_gate(t)
            less4 = rival(t, l4, "less4", 0, S)
            less5 = rival(t, l5, "less5", 0, S)
            pair_sum(t + 1, 0, S)
            z2_rows(t, 0, S, less4, less5)
            weight_steps[t]()

        st_and_gate(LAST)
        first4 = rival(LAST, l4, "less4", 0, HALF)
        first5 = rival(LAST, l5, "less5", 0, HALF)
        second4 = rival(LAST, l4, "less4", HALF, S)
        z2_rows(LAST, 0, HALF, first4, first5)
        second5 = rival(LAST, l5, "less5", HALF, S)
        round_z2(0, HALF)
        z2_rows(LAST, HALF, S, second4, second5)
        round_z2(HALF, S)

        round_z(0, HALF)
        quantise(z2_bf, z2_codes, z2_scales, 0, HALF)
        quantise(z_bf, z_first, z_scales, 0, HALF)
        round_z(HALF, S)
        quantise(z2_bf, z2_codes, z2_scales, HALF, S)
        z_second = keep.tile([P, S], U32, name="z2_bf", align_bytes=64)
        quantise(z_bf, z_second, z_scales, HALF, S)

        w23_later = keep.tile([P, 2 * N], U32, name="z_bf", align_bytes=64)
        quantise(w23_bf, w23_later, w23_scales, 2 * P, N)
        quantise(w23_bf, w23_later, w23_scales, N, 2 * N)

        pieces = [HALVES] + [((0, S),)] * LAST
        acc_h = [[psum.tile([P, c1 - c0], F32, name="acc") for c0, c1 in pieces[t]] for t in range(PACK)]
        for t in range(PACK):
            w_codes = w23_later if t else w23_first
            for c, (c0, c1) in enumerate(HALVES):
                acc = acc_h[t][0][:, c0:c1] if t else acc_h[0][c][:]
                z_codes = z_second if c else z_first
                product(acc, w_codes, w23_scales, 2 * t, z2_codes[:, c0:c1], z2_scales[:, c0:c1], True, False)
                product(acc, w_codes, w23_scales, 2 * t + 1, z_codes[:, c0:c1], z_scales[:, c0:c1], False, True)

        for t in range(PACK):
            for acc, (c0, c1) in zip(acc_h[t], pieces[t]):
                nc.scalar.activation(window[t][:, c0:c1], acc[:], ACT.Relu)
            for acc, (c0, c1) in zip(acc_h[t], pieces[t]):
                nc.scalar.copy(plain[t][:, c0:c1], acc[:])

        out_rows = out.rearrange("(p t) u -> p t u", t=PACK)

        def fetch(t):
            minus = ring.tile([P, S], F32, name="minus")
            nc.vector.tensor_scalar(minus[:], window[t][:].indirect(l7[:]), -1.0, 0.0, ALU.mult, ALU.add)
            return minus

        def put(t, minus):
            nc.vector.tensor_tensor(page[t][:].indirect(l6[:]), plain[t], minus[:], ALU.add)
            nc.sync.dma_start(out_rows[:, t, :], page[t][:])

        put(0, fetch(0))
        minus = fetch(1)
        for t in range(1, LAST):
            ahead = fetch(t + 1)
            put(t, minus)
            minus = ahead
        put(LAST, minus)
